import numpy as np
import ml_dtypes


def mxq(x, axis, fmt="e4m3"):
    dtype, down = {"e4m3": (ml_dtypes.float8_e4m3fn, 7), "e5m2": (ml_dtypes.float8_e5m2, 14)}[fmt]
    v = np.moveaxis(np.asarray(x, np.float32).astype(ml_dtypes.bfloat16).astype(np.float64), axis, -1)
    blocks = v.reshape(v.shape[:-1] + (-1, 32))
    amax = np.abs(blocks).max(-1, keepdims=True)
    byte = np.maximum(np.where(amax > 0, np.frexp(amax)[1] - 1 + 127, 0) - down, 1)
    scale = np.exp2(byte - 127.0)
    codes = (blocks / scale).astype(np.float32).astype(dtype).astype(np.float64)
    return np.moveaxis((codes * scale).reshape(v.shape), -1, axis)


WIDE = False


def mx_kscale(k):
    if not WIDE:
        return np.ones(k)
    levels = np.array([10, -10, 5, -5, 0])
    if k % 512:
        return np.exp2(np.random.permutation(np.resize(levels, k // 32))).repeat(32)
    a = np.empty((k // 512, 16))
    for p in range(k // 512):
        a[p, :8] = np.random.permutation(np.resize(levels, 8))
        for g in range(8):
            far = levels[np.abs(levels - a[p, g]) >= 10]
            a[p, g + 8] = far[np.random.randint(len(far))]
    return np.exp2(a.ravel()).repeat(32)


def f64(x):
    return np.asarray(x).astype(np.float64)


def striped8(idx):
    return np.asarray(idx).reshape(8, -1, 16).transpose(0, 2, 1).reshape(128, -1).astype(np.uint16)


def unstriped8(offs):
    return offs.reshape(8, 16, -1).transpose(0, 2, 1).reshape(8, -1).astype(np.int64)


def pick8(x, idx, run):
    r = np.arange(len(x))
    return x[r[:, None], idx[r % (8 * run) // run]]


E2M1 = np.array([0.0, 0.5, 1.0, 1.5, 2.0, 3.0, 4.0, 6.0, -0.0, -0.5, -1.0, -1.5, -2.0, -3.0, -4.0, -6.0])


def pack_weight(w, fmt):
    k, n = w.shape
    w = f64(np.asarray(w, np.float32).astype(ml_dtypes.bfloat16)).reshape(k // 32, 32, n)
    amax = np.abs(w).max(1)
    if fmt == "e4m3":
        byte = np.frexp(amax)[1] - 1 + 127 - 7
    else:
        mant, ex = np.frexp(amax / 6.0)
        byte = np.where(mant > 0.5, ex, ex - 1) + 127
    byte = np.clip(np.where(amax > 0, byte, 1), 1, 254)
    scaled = (w * np.exp2(127.0 - byte)[:, None, :]).reshape(k, n).astype(np.float32)
    by_word = np.ascontiguousarray(scaled.reshape(k // 512, 128, 4, n).transpose(0, 1, 3, 2))
    if fmt == "e4m3":
        words = by_word.astype(ml_dtypes.float8_e4m3fn).view(np.uint8)
    else:
        c = by_word.astype(ml_dtypes.float4_e2m1fn).view(np.uint8) & 0xF
        words = (c[..., 0::2] | (c[..., 1::2] << 4)).reshape(k // 512, 128, 2 * n)
    return np.ascontiguousarray(words), np.ascontiguousarray(byte.astype(np.uint8).reshape(k // 512, 16, n))


def unpack_weight(words, scales, fmt):
    g, _, n = scales.shape
    words = np.ascontiguousarray(words).reshape(g, 128, n, -1)
    if fmt == "e4m3":
        vals = words.view(ml_dtypes.float8_e4m3fn).astype(np.float64)
    else:
        nib = np.empty((g, 128, n, 4), np.uint8)
        nib[..., 0::2] = words & 0xF
        nib[..., 1::2] = words >> 4
        vals = E2M1[nib]
    vals = vals * np.repeat(np.exp2(scales.astype(np.float64) - 127.0), 8, axis=1)[..., None]
    return vals.transpose(0, 1, 3, 2).reshape(g * 512, n)


D, V, Q, I = 512, 2048, 128, 512


def setup_inputs():
    n = np.random.standard_normal
    idx = np.stack([np.random.permutation(V)[:I] for _ in range(8)])
    idx2 = np.stack([np.random.permutation(V)[:I] for _ in range(8)])
    fd = mx_kscale(D)
    vocp = pack_weight(n((D, V)) / fd[:, None], "e4m3")
    return {
        "hid": (n((D, Q)) * 0.8 / np.sqrt(D) * fd[:, None]).astype(np.float32),
        "voc_words": vocp[0],
        "voc_scales": vocp[1],
        "target": (np.random.uniform(0.0, 2.0, (Q, I))).astype(np.float32),
        "dhid": (n((D, Q)) * 1.0 / np.sqrt(D) * fd[:, None]).astype(np.float32),
        "base": (0.5 * n((Q, V))).astype(np.float32),
        "offs": striped8(idx),
        "offs2": striped8(idx2),
    }


def reference(hid, voc_words, voc_scales, target, dhid, base, offs, offs2):
    idx = unstriped8(offs)
    idx2 = unstriped8(offs2)
    vocu = unpack_weight(voc_words, voc_scales, "e4m3")
    hidq = mxq(f64(hid), 0, "e4m3")
    a = hidq.T @ vocu
    dhidq = mxq(f64(dhid), 0, "e4m3")
    ta = dhidq.T @ vocu
    p = np.exp(pick8(a, idx, 16))
    z = np.sum(p, axis=1, keepdims=True)
    b = np.exp(pick8(a, idx2, 16)) / z * 512.0
    db = f64(target) / (b + 1.0)
    dz = np.sum(db * 512.0 * np.exp(pick8(a, idx2, 16)) / np.square(z) * (-1.0), axis=1, keepdims=True)
    xp = pick8(ta, idx, 16) * p
    xz = np.sum(xp, axis=1, keepdims=True)
    xb = (pick8(ta, idx2, 16) * np.exp(pick8(a, idx2, 16)) - xz * np.exp(pick8(a, idx2, 16)) / z) / z * 512.0
    xdb = xb * f64(target) / np.square(b + 1.0) * (-1.0)
    xdz = np.sum((xdb * 512.0 * np.exp(pick8(a, idx2, 16)) + pick8(ta, idx2, 16) * np.exp(pick8(a, idx2, 16)) * db * 512.0 - xz * z * 2.0 * db * 512.0 * np.exp(pick8(a, idx2, 16)) / np.square(z)) / np.square(z) * (-1.0), axis=1, keepdims=True)
    xe1 = (xdb * 512.0 - xz * db * 512.0 / z) / z * np.exp(pick8(a, idx2, 16)) + pick8(ta, idx2, 16) * np.exp(pick8(a, idx2, 16)) * db * 512.0 / z
    xs1 = np.zeros((Q, V))
    xs1[np.arange(Q)[:, None], idx2[np.arange(Q) % 128 // 16]] = xe1
    xe2 = xdz * p + xp * dz
    xs2 = np.zeros((Q, V))
    xs2[np.arange(Q)[:, None], idx[np.arange(Q) % 128 // 16]] = xe2
    xda = xs1 + xs2
    y = xda + f64(base)
    return y

@@ -1,0 +1,223 @@
+import math
+from contextlib import ExitStack
+
+import concourse.mybir as mybir
+from concourse.masks import make_identity
+
+D, V, Q, I = 512, 2048, 128, 512
+FLOPS = 2 * 2 * D * Q * V
+
+F32 = mybir.dt.float32
+BF16 = mybir.dt.bfloat16
+I32 = mybir.dt.int32
+U32 = mybir.dt.uint32
+U16 = mybir.dt.uint16
+U8 = mybir.dt.uint8
+FP8X4 = mybir.dt.float8_e4m3fn_x4
+ALU = mybir.AluOpType
+ACT = mybir.ActivationFunctionType
+AXIS = mybir.AxisListType
+
+P = 128
+PACK = 4
+BANK = 512
+SCORE_CHUNKS = ((0, 512), (512, 1024), (1024, 1536), (1536, 1792), (1792, 2048))
+LOAD_CHUNKS = ((0, 1024), (1024, 1536), (1536, 2048))
+STORE_CHUNKS = ((0, 256), (256, 512), (512, 1024), (1024, 1536), (1536, 1792), (1792, 2048))
+LN2 = math.log(2.0)
+BITS_TO_LN = LN2 / 2.0**23
+BITS_OFFSET = (127.0 - 0.043) * LN2
+
+
+def tile_attend_hvallowed_heads_kernel(tc, hid, voc_words, voc_scales, target, dhid, base, offs, offs2, out):
+    nc = tc.nc
+    with ExitStack() as ctx:
+        lists = ctx.enter_context(tc.tile_pool(name="lists", bufs=1))
+        sb = ctx.enter_context(tc.tile_pool(name="sb", bufs=1))
+        psum = ctx.enter_context(tc.psum_pool(name="psum", bufs=1))
+
+        def bank(number, width, name):
+            return psum.tile([P, width], F32, name=name, tag="bank%d" % number)
+
+        def column(name):
+            return sb.tile([P, 1], F32, name=name)
+
+        def row(name):
+            return sb.tile([P, I], F32, name=name)
+
+        allowed = lists.tile([P, I // 16], U16, name="allowed")
+        scored = lists.tile([P, I // 16], U16, name="scored")
+
+        voc_scale = sb.tile([P, BANK], U8, name="voc_scale", align_bytes=64)
+        nc.gpsimd.memset(voc_scale[:].bitcast(I32), 0)
+        hid_raw = sb.tile([P, PACK, Q], F32, name="hid_raw")
+        dhid_raw = sb.tile([P, PACK, Q], F32, name="dhid_raw")
+        nc.sync.dma_start(out=hid_raw[:], in_=hid.rearrange("(p j) q -> p j q", j=PACK))
+        scales_hbm = voc_scales[0].bitcast(I32).rearrange("r (c w) -> c r w", c=4)
+        for quadrant in range(4):
+            nc.sync.dma_start(
+                out=voc_scale[32 * quadrant : 32 * quadrant + 16, :].bitcast(I32),
+                in_=scales_hbm[:, 4 * quadrant : 4 * quadrant + 4, :],
+            )
+        words_hbm = voc_words[0].rearrange("p n t -> p (n t)")
+        words = []
+        for c, (lo, hi) in enumerate(LOAD_CHUNKS):
+            if c == len(LOAD_CHUNKS) - 1:
+                nc.sync.dma_start(out=dhid_raw[:], in_=dhid.rearrange("(p j) q -> p j q", j=PACK))
+            chunk = sb.tile([P, hi - lo], U32, name="words%d" % c, align_bytes=64)
+            nc.sync.dma_start(out=chunk[:].bitcast(I32), in_=words_hbm[:, PACK * lo : PACK * hi].bitcast(I32))
+            words.append(chunk)
+        nc.sync.dma_start(allowed[:], offs)
+        nc.sync.dma_start(scored[:], offs2)
+        weight = row("weight")
+        nc.sync.dma_start(out=weight[:], in_=target)
+        base_sb = sb.tile([P, V], F32, name="base_sb")
+        nc.sync.dma_start(out=base_sb[:], in_=base)
+
+        one = column("one")
+        nc.gpsimd.memset(one[:], 1.0)
+        minus_two = column("minus_two")
+        nc.scalar.activation(minus_two[:], one[:], ACT.Identity, scale=-2.0)
+        ident = sb.tile([P, P], F32, name="ident")
+        make_identity(nc, ident[:])
+
+        xs1 = sb.tile([P, V], F32, name="xs1")
+        nc.vector.memset(xs1[:], 0.0)
+
+        def quantise(raw, name):
+            grouped = sb.tile([P, Q, PACK], BF16, name=name + "_bf16", align_bytes=64)
+            codes = sb.tile([P, Q], U32, name=name + "_codes", align_bytes=64)
+            scale = sb.tile([P, Q], U8, name=name + "_scale", align_bytes=64)
+            nc.vector.tensor_copy(
+                out=grouped[:].rearrange("p (c i) t -> p c t i", i=4),
+                in_=raw[:].rearrange("p t (c i) -> p c t i", i=4),
+            )
+            nc.vector.quantize_mx(
+                out=codes[:].bitcast(FP8X4), scales=scale[:], in_=grouped[:].rearrange("p q t -> p (q t)")
+            )
+            return codes, scale
+
+        hid_mx = quantise(hid_raw, "hid")
+        dhid_mx = quantise(dhid_raw, "dhid")
+
+        def scores(acc, stationary, c):
+            lo, hi = SCORE_CHUNKS[c]
+            load = [k for k, (first, end) in enumerate(LOAD_CHUNKS) if first <= lo < end][0]
+            first = LOAD_CHUNKS[load][0]
+            plane = lo // BANK
+            nc.tensor.matmul_mx(
+                out=acc,
+                lhsT=stationary[0][:].bitcast(FP8X4),
+                lhsT_scale=stationary[1][:],
+                rhs=words[load][:, lo - first : hi - first].bitcast(FP8X4),
+                rhs_scale=voc_scale[4 * plane :, lo - plane * BANK : hi - plane * BANK],
+                start=True,
+                stop=True,
+            )
+
+        a = sb.tile([P, V], F32, name="a")
+        ta = sb.tile([P, V], F32, name="ta", tag="wide")
+        for c, (lo, hi) in enumerate(SCORE_CHUNKS):
+            acc = bank(c, hi - lo, "a_acc%d" % c)
+            scores(acc[:], hid_mx, c)
+            if c % 2 == 0:
+                nc.scalar.copy(a[:, lo:hi], acc[:])
+            else:
+                nc.vector.tensor_copy(a[:, lo:hi], acc[:])
+        ta_acc = []
+        for b in range(4):
+            acc = bank((5 + b) % 8, BANK, "ta_acc%d" % b)
+            for c, (lo, hi) in enumerate(SCORE_CHUNKS):
+                if lo // BANK == b:
+                    scores(acc[:, lo - b * BANK : hi - b * BANK], dhid_mx, c)
+            ta_acc.append(acc)
+            if b < 3:
+                nc.scalar.copy(ta[:, b * BANK : (b + 1) * BANK], acc[:])
+
+        a1 = row("a1")
+        nc.vector.tensor_copy(a1[:], a[:].indirect(allowed[:]))
+        neg_max = column("neg_max")
+        nc.vector.tensor_reduce(neg_max[:], a1[:], AXIS.X, ALU.max, negate=True)
+        p = row("p")
+        z = column("z")
+        nc.scalar.activation(p[:], a1[:], ACT.Exp, bias=neg_max[:], accum_out=z[:])
+        nc.scalar.copy(ta[:, 3 * BANK :], ta_acc[3][:])
+        a2 = row("a2")
+        nc.vector.tensor_copy(a2[:], a[:].indirect(scored[:]))
+
+        k0 = column("k0")
+        nc.scalar.activation(k0[:], neg_max[:], ACT.Identity, scale=0.5, bias=(math.log(512.0) - 0.5) / 2)
+        z_bits = z[:].bitcast(U32)
+        e0, n0, q0, k1, e1, k2, q1, shift = (column(n) for n in ("e0", "n0", "q0", "k1", "e1", "k2", "q1", "shift"))
+        nc.scalar.activation(e0[:], z_bits, ACT.Exp, scale=-BITS_TO_LN, bias=BITS_OFFSET)
+        nc.scalar.activation(n0[:], z_bits, ACT.Identity, scale=-BITS_TO_LN, bias=BITS_OFFSET - 0.5)
+        nc.scalar.activation(q0[:], e0[:], ACT.Square, scale=z[:], bias=minus_two[:])
+        nc.scalar.activation(k1[:], n0[:], ACT.Identity, scale=0.5, bias=k0[:])
+        nc.scalar.activation(e1[:], q0[:], ACT.Exp, scale=0.5, bias=n0[:])
+        nc.scalar.activation(k2[:], q0[:], ACT.Identity, scale=0.25, bias=k1[:])
+        nc.scalar.activation(q1[:], e1[:], ACT.Square, scale=z[:], bias=minus_two[:])
+        nc.scalar.activation(shift[:], q1[:], ACT.Identity, scale=0.25, bias=k2[:])
+        th = row("th")
+        nc.scalar.activation(th[:], a2[:], ACT.Tanh, scale=0.5, bias=shift[:])
+        th_sq = row("th_sq")
+        nc.scalar.activation(th_sq[:], th[:], ACT.Square, scale=0.5)
+
+
+        t2 = row("t2")
+        nc.vector.tensor_scalar(t2[:], ta[:].indirect(scored[:]), -1.0, 0.0, ALU.mult, ALU.add)
+        rz = column("rz")
+        nc.vector.reciprocal(rz[:], z[:])
+        t1 = row("t1")
+        nc.vector.tensor_copy(t1[:], ta[:].indirect(allowed[:]))
+        xs2 = sb.tile([P, V], F32, name="xs2", tag="wide")
+        nc.gpsimd.memset(xs2[:], 0.0)
+        curve = row("curve")
+        nc.vector.scalar_tensor_tensor(curve[:], th_sq[:], 0.25, weight[:], ALU.subtract, ALU.mult)
+        mean = column("mean")
+        spent = row("spent")
+        nc.vector.scalar_tensor_tensor(spent[:], t1[:], rz[:], p[:], ALU.mult, ALU.mult, accum_out=mean[:])
+        g = column("g")
+        nc.vector.scalar_tensor_tensor(th_sq[:], th[:], 1.0, weight[:], ALU.add, ALU.mult, accum_out=g[:])
+        xe1 = row("xe1")
+        s1 = column("s1")
+        nc.vector.scalar_tensor_tensor(xe1[:], t2[:], mean[:], curve[:], ALU.add, ALU.mult, accum_out=s1[:])
+        nc.vector.tensor_copy(xs1[:].indirect(scored[:]), xe1[:])
+
+        gz, slope, part, minus_offset, offset = (column(n) for n in ("gz", "slope", "part", "minus_offset", "offset"))
+        nc.scalar.activation(gz[:], g[:], ACT.Identity, scale=rz[:])
+        nc.scalar.activation(slope[:], gz[:], ACT.Identity, scale=-0.5)
+        nc.scalar.activation(part[:], slope[:], ACT.Identity, scale=mean[:])
+        nc.scalar.activation(minus_offset[:], s1[:], ACT.Identity, scale=rz[:], bias=part[:])
+        nc.scalar.activation(offset[:], minus_offset[:], ACT.Identity, scale=-1.0)
+        f = row("f")
+        nc.scalar.activation(f[:], t1[:], ACT.Identity, scale=slope[:], bias=offset[:])
+        nc.vector.tensor_tensor(xs2[:].indirect(allowed[:]), f[:], p[:], ALU.mult)
+
+        blocks = BANK // P
+        turned = [bank(1 + b, BANK, "turned%d" % b) for b in range(3)]
+        for b in range(3):
+            for i in range(blocks):
+                cols = slice(b * BANK + i * P, b * BANK + (i + 1) * P)
+                nc.tensor.matmul(turned[b][:, i * P : (i + 1) * P], lhsT=base_sb[:, cols], rhs=ident[:],
+                                 start=(i == 0), stop=False, is_transpose=True)
+        partial = []
+        for b in range(3):
+            for i in range(blocks):
+                cols = slice(b * BANK + i * P, b * BANK + (i + 1) * P)
+                nc.tensor.matmul(turned[b][:, i * P : (i + 1) * P], lhsT=xs1[:, cols], rhs=ident[:],
+                                 start=False, stop=(i == blocks - 1), is_transpose=True)
+            turned_sb = sb.tile([P, BANK], F32, name="turned_sb%d" % b)
+            nc.scalar.copy(turned_sb[:], turned[b][:])
+            back = bank((5 + b) % 8, BANK, "back%d" % b)
+            for i in range(blocks):
+                nc.tensor.transpose(back[:, i * P : (i + 1) * P], turned_sb[:, i * P : (i + 1) * P], ident[:])
+            partial.append(back)
+        last = row("last")
+        nc.gpsimd.tensor_tensor(last[:], xs2[:, 3 * BANK :], base_sb[:, 3 * BANK :], ALU.add)
+        partial.append(last)
+
+        for c, (lo, hi) in enumerate(STORE_CHUNKS):
+            b = lo // BANK
+            result = sb.tile([P, hi - lo], F32, name="result%d" % c)
+            nc.vector.tensor_tensor(result[:], (xs2 if b < 3 else xs1)[:, lo:hi], partial[b][:, lo - b * BANK : hi - b * BANK], ALU.add)
+            nc.sync.dma_start(out=out[:, lo:hi], in_=result[:])

@@ -16,13 +16,12 @@ U8 = mybir.dt.uint8
 FP8X4 = mybir.dt.float8_e4m3fn_x4
 ALU = mybir.AluOpType
 ACT = mybir.ActivationFunctionType
-AXIS = mybir.AxisListType
 
 P = 128
 PACK = 4
 BANK = 512
 SCORE_CHUNKS = ((0, 512), (512, 1024), (1024, 1536), (1536, 1792), (1792, 2048))
-LOAD_CHUNKS = ((0, 1024), (1024, 1536), (1536, 2048))
+LOAD_CHUNKS = ((0, 512), (512, 1536), (1536, 2048))
 STORE_CHUNKS = ((0, 256), (256, 512), (512, 1024), (1024, 1536), (1536, 1792), (1792, 2048))
 LN2 = math.log(2.0)
 BITS_TO_LN = LN2 / 2.0**23
@@ -62,7 +61,7 @@ def tile_attend_hvallowed_heads_kernel(tc, hid, voc_words, voc_scales, target, d
         words_hbm = voc_words[0].rearrange("p n t -> p (n t)")
         words = []
         for c, (lo, hi) in enumerate(LOAD_CHUNKS):
-            if c == len(LOAD_CHUNKS) - 1:
+            if c == 2:
                 nc.sync.dma_start(out=dhid_raw[:], in_=dhid.rearrange("(p j) q -> p j q", j=PACK))
             chunk = sb.tile([P, hi - lo], U32, name="words%d" % c, align_bytes=64)
             nc.sync.dma_start(out=chunk[:].bitcast(I32), in_=words_hbm[:, PACK * lo : PACK * hi].bitcast(I32))
@@ -131,18 +130,18 @@ def tile_attend_hvallowed_heads_kernel(tc, hid, voc_words, voc_scales, target, d
                 if lo // BANK == b:
                     scores(acc[:, lo - b * BANK : hi - b * BANK], dhid_mx, c)
             ta_acc.append(acc)
-            if b < 3:
+            if b < 4:
                 nc.scalar.copy(ta[:, b * BANK : (b + 1) * BANK], acc[:])
 
         a1 = row("a1")
         nc.vector.tensor_copy(a1[:], a[:].indirect(allowed[:]))
         neg_max = column("neg_max")
-        nc.vector.tensor_reduce(neg_max[:], a1[:], AXIS.X, ALU.max, negate=True)
+        neg_a1 = row("neg_a1")
+        nc.vector.tensor_scalar(neg_a1[:], a1[:], -1.0, None, ALU.mult, ALU.min, accum_out=neg_max[:])
         p = row("p")
         z = column("z")
-        nc.scalar.activation(p[:], a1[:], ACT.Exp, bias=neg_max[:], accum_out=z[:])
-        nc.scalar.copy(ta[:, 3 * BANK :], ta_acc[3][:])
-        a2 = row("a2")
+        nc.scalar.activation(p[:], neg_a1[:], ACT.Exp, scale=-1.0, bias=neg_max[:], accum_out=z[:])
+        a2 = sb.tile([P, I], F32, name="a2", tag="a1")
         nc.vector.tensor_copy(a2[:], a[:].indirect(scored[:]))
 
         k0 = column("k0")
@@ -163,19 +162,19 @@ def tile_attend_hvallowed_heads_kernel(tc, hid, voc_words, voc_scales, target, d
         nc.scalar.activation(th_sq[:], th[:], ACT.Square, scale=0.5)
 
 
-        t2 = row("t2")
-        nc.vector.tensor_scalar(t2[:], ta[:].indirect(scored[:]), -1.0, 0.0, ALU.mult, ALU.add)
-        rz = column("rz")
-        nc.vector.reciprocal(rz[:], z[:])
         t1 = row("t1")
         nc.vector.tensor_copy(t1[:], ta[:].indirect(allowed[:]))
+        rz = column("rz")
+        nc.vector.reciprocal(rz[:], z[:])
+        t2 = row("t2")
+        nc.vector.tensor_scalar(t2[:], ta[:].indirect(scored[:]), -1.0, 0.0, ALU.mult, ALU.add)
         xs2 = sb.tile([P, V], F32, name="xs2", tag="wide")
         nc.gpsimd.memset(xs2[:], 0.0)
-        curve = row("curve")
-        nc.vector.scalar_tensor_tensor(curve[:], th_sq[:], 0.25, weight[:], ALU.subtract, ALU.mult)
         mean = column("mean")
         spent = row("spent")
         nc.vector.scalar_tensor_tensor(spent[:], t1[:], rz[:], p[:], ALU.mult, ALU.mult, accum_out=mean[:])
+        curve = row("curve")
+        nc.vector.scalar_tensor_tensor(curve[:], th_sq[:], 0.25, weight[:], ALU.subtract, ALU.mult)
         g = column("g")
         nc.vector.scalar_tensor_tensor(th_sq[:], th[:], 1.0, weight[:], ALU.add, ALU.mult, accum_out=g[:])
         xe1 = row("xe1")
@@ -216,8 +215,9 @@ def tile_attend_hvallowed_heads_kernel(tc, hid, voc_words, voc_scales, target, d
         nc.gpsimd.tensor_tensor(last[:], xs2[:, 3 * BANK :], base_sb[:, 3 * BANK :], ALU.add)
         partial.append(last)
 
-        for c, (lo, hi) in enumerate(STORE_CHUNKS):
+        results = [sb.tile([P, BANK], F32, name="result%d" % b, tag="turned_sb2" if b == 3 else "result%d" % b) for b in range(4)]
+        for lo, hi in STORE_CHUNKS:
             b = lo // BANK
-            result = sb.tile([P, hi - lo], F32, name="result%d" % c)
-            nc.vector.tensor_tensor(result[:], (xs2 if b < 3 else xs1)[:, lo:hi], partial[b][:, lo - b * BANK : hi - b * BANK], ALU.add)
-            nc.sync.dma_start(out=out[:, lo:hi], in_=result[:])
+            cols = slice(lo - b * BANK, hi - b * BANK)
+            nc.vector.tensor_tensor(results[b][:, cols], (xs2 if b < 3 else xs1)[:, lo:hi], partial[b][:, cols], ALU.add)
+            nc.sync.dma_start(out=out[:, lo:hi], in_=results[b][:, cols])

@@ -22,7 +22,7 @@ PACK = 4
 BANK = 512
 SCORE_CHUNKS = ((0, 512), (512, 1024), (1024, 1536), (1536, 1792), (1792, 2048))
 LOAD_CHUNKS = ((0, 512), (512, 1536), (1536, 2048))
-STORE_CHUNKS = ((0, 256), (256, 512), (512, 1024), (1024, 1536), (1536, 1792), (1792, 2048))
+STORE_CHUNKS = ((0, 128), (128, 512), (512, 1024), (1024, 1536), (1536, 1792), (1792, 2048))
 LN2 = math.log(2.0)
 BITS_TO_LN = LN2 / 2.0**23
 BITS_OFFSET = (127.0 - 0.043) * LN2
@@ -77,11 +77,12 @@ def tile_attend_hvallowed_heads_kernel(tc, hid, voc_words, voc_scales, target, d
         nc.gpsimd.memset(one[:], 1.0)
         minus_two = column("minus_two")
         nc.scalar.activation(minus_two[:], one[:], ACT.Identity, scale=-2.0)
-        ident = sb.tile([P, P], F32, name="ident")
-        make_identity(nc, ident[:])
 
         xs1 = sb.tile([P, V], F32, name="xs1")
-        nc.vector.memset(xs1[:], 0.0)
+        nc.vector.memset(xs1[:, : V - 1], 0.0)
+        nc.vector.memset(xs1[:, V - 1 :], 0.0)
+        xs2 = sb.tile([P, V], F32, name="xs2")
+        nc.gpsimd.memset(xs2[:], 0.0)
 
         def quantise(raw, name):
             grouped = sb.tile([P, Q, PACK], BF16, name=name + "_bf16", align_bytes=64)
@@ -97,6 +98,8 @@ def tile_attend_hvallowed_heads_kernel(tc, hid, voc_words, voc_scales, target, d
             return codes, scale
 
         hid_mx = quantise(hid_raw, "hid")
+        ident = sb.tile([P, P], F32, name="ident", tag="hid_bf16", align_bytes=64)
+        make_identity(nc, ident[:])
         dhid_mx = quantise(dhid_raw, "dhid")
 
         def scores(acc, stationary, c):
@@ -115,7 +118,7 @@ def tile_attend_hvallowed_heads_kernel(tc, hid, voc_words, voc_scales, target, d
             )
 
         a = sb.tile([P, V], F32, name="a")
-        ta = sb.tile([P, V], F32, name="ta", tag="wide")
+        ta = sb.tile([P, V], F32, name="ta")
         for c, (lo, hi) in enumerate(SCORE_CHUNKS):
             acc = bank(c, hi - lo, "a_acc%d" % c)
             scores(acc[:], hid_mx, c)
@@ -162,34 +165,36 @@ def tile_attend_hvallowed_heads_kernel(tc, hid, voc_words, voc_scales, target, d
         nc.scalar.activation(th_sq[:], th[:], ACT.Square, scale=0.5)
 
 
+        share = row("share")
+        nc.scalar.activation(share[:], th[:], ACT.Identity, scale=0.5, bias=0.5)
         t1 = row("t1")
         nc.vector.tensor_copy(t1[:], ta[:].indirect(allowed[:]))
         rz = column("rz")
         nc.vector.reciprocal(rz[:], z[:])
         t2 = row("t2")
         nc.vector.tensor_scalar(t2[:], ta[:].indirect(scored[:]), -1.0, 0.0, ALU.mult, ALU.add)
-        xs2 = sb.tile([P, V], F32, name="xs2", tag="wide")
-        nc.gpsimd.memset(xs2[:], 0.0)
         mean = column("mean")
         spent = row("spent")
         nc.vector.scalar_tensor_tensor(spent[:], t1[:], rz[:], p[:], ALU.mult, ALU.mult, accum_out=mean[:])
         curve = row("curve")
         nc.vector.scalar_tensor_tensor(curve[:], th_sq[:], 0.25, weight[:], ALU.subtract, ALU.mult)
-        g = column("g")
-        nc.vector.scalar_tensor_tensor(th_sq[:], th[:], 1.0, weight[:], ALU.add, ALU.mult, accum_out=g[:])
         xe1 = row("xe1")
         s1 = column("s1")
         nc.vector.scalar_tensor_tensor(xe1[:], t2[:], mean[:], curve[:], ALU.add, ALU.mult, accum_out=s1[:])
         nc.vector.tensor_copy(xs1[:].indirect(scored[:]), xe1[:])
 
-        gz, slope, part, minus_offset, offset = (column(n) for n in ("gz", "slope", "part", "minus_offset", "offset"))
-        nc.scalar.activation(gz[:], g[:], ACT.Identity, scale=rz[:])
-        nc.scalar.activation(slope[:], gz[:], ACT.Identity, scale=-0.5)
-        nc.scalar.activation(part[:], slope[:], ACT.Identity, scale=mean[:])
-        nc.scalar.activation(minus_offset[:], s1[:], ACT.Identity, scale=rz[:], bias=part[:])
-        nc.scalar.activation(offset[:], minus_offset[:], ACT.Identity, scale=-1.0)
+        minus_rz = sb.tile([P, 1], F32, name="minus_rz", tag="shift")
+        nc.scalar.activation(minus_rz[:], rz[:], ACT.Identity, scale=-1.0)
+        minus_rz_mean, offset, minus_g = (column(n) for n in ("minus_rz_mean", "offset", "minus_g"))
+        nc.scalar.activation(minus_rz_mean[:], mean[:], ACT.Identity, scale=minus_rz[:])
+        centred = row("centred")
+        nc.scalar.activation(centred[:], t1[:], ACT.Identity, scale=rz[:], bias=minus_rz_mean[:])
+        nc.scalar.activation(offset[:], s1[:], ACT.Identity, scale=minus_rz[:])
+        weighted = sb.tile([P, I], F32, name="weighted", tag="curve")
+        nc.gpsimd.tensor_tensor(weighted[:], share[:], weight[:], ALU.mult)
+        nc.scalar.activation(spent[:], weighted[:], ACT.Identity, scale=-1.0, accum_out=minus_g[:])
         f = row("f")
-        nc.scalar.activation(f[:], t1[:], ACT.Identity, scale=slope[:], bias=offset[:])
+        nc.scalar.activation(f[:], centred[:], ACT.Identity, scale=minus_g[:], bias=offset[:])
         nc.vector.tensor_tensor(xs2[:].indirect(allowed[:]), f[:], p[:], ALU.mult)
 
         blocks = BANK // P
@@ -200,22 +205,22 @@ def tile_attend_hvallowed_heads_kernel(tc, hid, voc_words, voc_scales, target, d
                 nc.tensor.matmul(turned[b][:, i * P : (i + 1) * P], lhsT=base_sb[:, cols], rhs=ident[:],
                                  start=(i == 0), stop=False, is_transpose=True)
         partial = []
+        turned_sb = sb.tile([P, 3 * BANK], F32, name="turned_sb", tag="centred")
         for b in range(3):
             for i in range(blocks):
                 cols = slice(b * BANK + i * P, b * BANK + (i + 1) * P)
                 nc.tensor.matmul(turned[b][:, i * P : (i + 1) * P], lhsT=xs1[:, cols], rhs=ident[:],
                                  start=False, stop=(i == blocks - 1), is_transpose=True)
-            turned_sb = sb.tile([P, BANK], F32, name="turned_sb%d" % b)
-            nc.scalar.copy(turned_sb[:], turned[b][:])
+            nc.scalar.copy(turned_sb[:, b * BANK : (b + 1) * BANK], turned[b][:])
             back = bank((5 + b) % 8, BANK, "back%d" % b)
             for i in range(blocks):
-                nc.tensor.transpose(back[:, i * P : (i + 1) * P], turned_sb[:, i * P : (i + 1) * P], ident[:])
+                nc.tensor.transpose(back[:, i * P : (i + 1) * P], turned_sb[:, b * BANK + i * P : b * BANK + (i + 1) * P], ident[:])
             partial.append(back)
         last = row("last")
         nc.gpsimd.tensor_tensor(last[:], xs2[:, 3 * BANK :], base_sb[:, 3 * BANK :], ALU.add)
         partial.append(last)
 
-        results = [sb.tile([P, BANK], F32, name="result%d" % b, tag="turned_sb2" if b == 3 else "result%d" % b) for b in range(4)]
+        results = [sb.tile([P, BANK], F32, name="result%d" % b, tag="centred" if b == 3 else "result%d" % b) for b in range(4)]
         for lo, hi in STORE_CHUNKS:
             b = lo // BANK
             cols = slice(lo - b * BANK, hi - b * BANK)

import math
from contextlib import ExitStack

import concourse.mybir as mybir
from concourse.masks import make_identity

D, V, Q, I = 512, 2048, 128, 512
FLOPS = 2 * 2 * D * Q * V

F32 = mybir.dt.float32
BF16 = mybir.dt.bfloat16
I32 = mybir.dt.int32
U32 = mybir.dt.uint32
U16 = mybir.dt.uint16
U8 = mybir.dt.uint8
FP8X4 = mybir.dt.float8_e4m3fn_x4
ALU = mybir.AluOpType
ACT = mybir.ActivationFunctionType

P = 128
PACK = 4
BANK = 512
SCORE_CHUNKS = ((0, 512), (512, 1024), (1024, 1536), (1536, 1792), (1792, 2048))
LOAD_CHUNKS = ((0, 512), (512, 1536), (1536, 2048))
STORE_CHUNKS = ((0, 128), (128, 512), (512, 1024), (1024, 1536), (1536, 1792), (1792, 2048))
LN2 = math.log(2.0)
BITS_TO_LN = LN2 / 2.0**23
BITS_OFFSET = (127.0 - 0.043) * LN2


def tile_attend_hvallowed_heads_kernel(tc, hid, voc_words, voc_scales, target, dhid, base, offs, offs2, out):
    nc = tc.nc
    with ExitStack() as ctx:
        lists = ctx.enter_context(tc.tile_pool(name="lists", bufs=1))
        sb = ctx.enter_context(tc.tile_pool(name="sb", bufs=1))
        psum = ctx.enter_context(tc.psum_pool(name="psum", bufs=1))

        def bank(number, width, name):
            return psum.tile([P, width], F32, name=name, tag="bank%d" % number)

        def column(name):
            return sb.tile([P, 1], F32, name=name)

        def row(name):
            return sb.tile([P, I], F32, name=name)

        allowed = lists.tile([P, I // 16], U16, name="allowed")
        scored = lists.tile([P, I // 16], U16, name="scored")

        voc_scale = sb.tile([P, BANK], U8, name="voc_scale", align_bytes=64)
        nc.gpsimd.memset(voc_scale[:].bitcast(I32), 0)
        hid_raw = sb.tile([P, PACK, Q], F32, name="hid_raw")
        dhid_raw = sb.tile([P, PACK, Q], F32, name="dhid_raw")
        nc.sync.dma_start(out=hid_raw[:], in_=hid.rearrange("(p j) q -> p j q", j=PACK))
        scales_hbm = voc_scales[0].bitcast(I32).rearrange("r (c w) -> c r w", c=4)
        for quadrant in range(4):
            nc.sync.dma_start(
                out=voc_scale[32 * quadrant : 32 * quadrant + 16, :].bitcast(I32),
                in_=scales_hbm[:, 4 * quadrant : 4 * quadrant + 4, :],
            )
        words_hbm = voc_words[0].rearrange("p n t -> p (n t)")
        words = []
        for c, (lo, hi) in enumerate(LOAD_CHUNKS):
            if c == 2:
                nc.sync.dma_start(out=dhid_raw[:], in_=dhid.rearrange("(p j) q -> p j q", j=PACK))
            chunk = sb.tile([P, hi - lo], U32, name="words%d" % c, align_bytes=64)
            nc.sync.dma_start(out=chunk[:].bitcast(I32), in_=words_hbm[:, PACK * lo : PACK * hi].bitcast(I32))
            words.append(chunk)
        nc.sync.dma_start(allowed[:], offs)
        nc.sync.dma_start(scored[:], offs2)
        weight = row("weight")
        nc.sync.dma_start(out=weight[:], in_=target)
        base_sb = sb.tile([P, V], F32, name="base_sb")
        nc.sync.dma_start(out=base_sb[:], in_=base)

        one = column("one")
        nc.gpsimd.memset(one[:], 1.0)
        minus_two = column("minus_two")
        nc.scalar.activation(minus_two[:], one[:], ACT.Identity, scale=-2.0)

        xs1 = sb.tile([P, V], F32, name="xs1")
        nc.vector.memset(xs1[:, : V - 1], 0.0)
        nc.vector.memset(xs1[:, V - 1 :], 0.0)
        xs2 = sb.tile([P, V], F32, name="xs2")
        nc.gpsimd.memset(xs2[:], 0.0)

        def quantise(raw, name):
            grouped = sb.tile([P, Q, PACK], BF16, name=name + "_bf16", align_bytes=64)
            codes = sb.tile([P, Q], U32, name=name + "_codes", align_bytes=64)
            scale = sb.tile([P, Q], U8, name=name + "_scale", align_bytes=64)
            nc.vector.tensor_copy(
                out=grouped[:].rearrange("p (c i) t -> p c t i", i=4),
                in_=raw[:].rearrange("p t (c i) -> p c t i", i=4),
            )
            nc.vector.quantize_mx(
                out=codes[:].bitcast(FP8X4), scales=scale[:], in_=grouped[:].rearrange("p q t -> p (q t)")
            )
            return codes, scale

        hid_mx = quantise(hid_raw, "hid")
        ident = sb.tile([P, P], F32, name="ident", tag="hid_bf16", align_bytes=64)
        make_identity(nc, ident[:])
        dhid_mx = quantise(dhid_raw, "dhid")

        def scores(acc, stationary, c):
            lo, hi = SCORE_CHUNKS[c]
            load = [k for k, (first, end) in enumerate(LOAD_CHUNKS) if first <= lo < end][0]
            first = LOAD_CHUNKS[load][0]
            plane = lo // BANK
            nc.tensor.matmul_mx(
                out=acc,
                lhsT=stationary[0][:].bitcast(FP8X4),
                lhsT_scale=stationary[1][:],
                rhs=words[load][:, lo - first : hi - first].bitcast(FP8X4),
                rhs_scale=voc_scale[4 * plane :, lo - plane * BANK : hi - plane * BANK],
                start=True,
                stop=True,
            )

        a = sb.tile([P, V], F32, name="a")
        ta = sb.tile([P, V], F32, name="ta")
        for c, (lo, hi) in enumerate(SCORE_CHUNKS):
            acc = bank(c, hi - lo, "a_acc%d" % c)
            scores(acc[:], hid_mx, c)
            if c % 2 == 0:
                nc.scalar.copy(a[:, lo:hi], acc[:])
            else:
                nc.vector.tensor_copy(a[:, lo:hi], acc[:])
        ta_acc = []
        for b in range(4):
            acc = bank((5 + b) % 8, BANK, "ta_acc%d" % b)
            for c, (lo, hi) in enumerate(SCORE_CHUNKS):
                if lo // BANK == b:
                    scores(acc[:, lo - b * BANK : hi - b * BANK], dhid_mx, c)
            ta_acc.append(acc)
            if b < 4:
                nc.scalar.copy(ta[:, b * BANK : (b + 1) * BANK], acc[:])

        a1 = row("a1")
        nc.vector.tensor_copy(a1[:], a[:].indirect(allowed[:]))
        neg_max = column("neg_max")
        neg_a1 = row("neg_a1")
        nc.vector.tensor_scalar(neg_a1[:], a1[:], -1.0, None, ALU.mult, ALU.min, accum_out=neg_max[:])
        p = row("p")
        z = column("z")
        nc.scalar.activation(p[:], neg_a1[:], ACT.Exp, scale=-1.0, bias=neg_max[:], accum_out=z[:])
        a2 = sb.tile([P, I], F32, name="a2", tag="a1")
        nc.vector.tensor_copy(a2[:], a[:].indirect(scored[:]))

        k0 = column("k0")
        nc.scalar.activation(k0[:], neg_max[:], ACT.Identity, scale=0.5, bias=(math.log(512.0) - 0.5) / 2)
        z_bits = z[:].bitcast(U32)
        e0, n0, q0, k1, e1, k2, q1, shift = (column(n) for n in ("e0", "n0", "q0", "k1", "e1", "k2", "q1", "shift"))
        nc.scalar.activation(e0[:], z_bits, ACT.Exp, scale=-BITS_TO_LN, bias=BITS_OFFSET)
        nc.scalar.activation(n0[:], z_bits, ACT.Identity, scale=-BITS_TO_LN, bias=BITS_OFFSET - 0.5)
        nc.scalar.activation(q0[:], e0[:], ACT.Square, scale=z[:], bias=minus_two[:])
        nc.scalar.activation(k1[:], n0[:], ACT.Identity, scale=0.5, bias=k0[:])
        nc.scalar.activation(e1[:], q0[:], ACT.Exp, scale=0.5, bias=n0[:])
        nc.scalar.activation(k2[:], q0[:], ACT.Identity, scale=0.25, bias=k1[:])
        nc.scalar.activation(q1[:], e1[:], ACT.Square, scale=z[:], bias=minus_two[:])
        nc.scalar.activation(shift[:], q1[:], ACT.Identity, scale=0.25, bias=k2[:])
        th = row("th")
        nc.scalar.activation(th[:], a2[:], ACT.Tanh, scale=0.5, bias=shift[:])
        th_sq = row("th_sq")
        nc.scalar.activation(th_sq[:], th[:], ACT.Square, scale=0.5)


        share = row("share")
        nc.scalar.activation(share[:], th[:], ACT.Identity, scale=0.5, bias=0.5)
        t1 = row("t1")
        nc.vector.tensor_copy(t1[:], ta[:].indirect(allowed[:]))
        rz = column("rz")
        nc.vector.reciprocal(rz[:], z[:])
        t2 = row("t2")
        nc.vector.tensor_scalar(t2[:], ta[:].indirect(scored[:]), -1.0, 0.0, ALU.mult, ALU.add)
        mean = column("mean")
        spent = row("spent")
        nc.vector.scalar_tensor_tensor(spent[:], t1[:], rz[:], p[:], ALU.mult, ALU.mult, accum_out=mean[:])
        curve = row("curve")
        nc.vector.scalar_tensor_tensor(curve[:], th_sq[:], 0.25, weight[:], ALU.subtract, ALU.mult)
        xe1 = row("xe1")
        s1 = column("s1")
        nc.vector.scalar_tensor_tensor(xe1[:], t2[:], mean[:], curve[:], ALU.add, ALU.mult, accum_out=s1[:])
        nc.vector.tensor_copy(xs1[:].indirect(scored[:]), xe1[:])

        minus_rz = sb.tile([P, 1], F32, name="minus_rz", tag="shift")
        nc.scalar.activation(minus_rz[:], rz[:], ACT.Identity, scale=-1.0)
        minus_rz_mean, offset, minus_g = (column(n) for n in ("minus_rz_mean", "offset", "minus_g"))
        nc.scalar.activation(minus_rz_mean[:], mean[:], ACT.Identity, scale=minus_rz[:])
        centred = row("centred")
        nc.scalar.activation(centred[:], t1[:], ACT.Identity, scale=rz[:], bias=minus_rz_mean[:])
        nc.scalar.activation(offset[:], s1[:], ACT.Identity, scale=minus_rz[:])
        weighted = sb.tile([P, I], F32, name="weighted", tag="curve")
        nc.gpsimd.tensor_tensor(weighted[:], share[:], weight[:], ALU.mult)
        nc.scalar.activation(spent[:], weighted[:], ACT.Identity, scale=-1.0, accum_out=minus_g[:])
        f = row("f")
        nc.scalar.activation(f[:], centred[:], ACT.Identity, scale=minus_g[:], bias=offset[:])
        nc.vector.tensor_tensor(xs2[:].indirect(allowed[:]), f[:], p[:], ALU.mult)

        blocks = BANK // P
        turned = [bank(1 + b, BANK, "turned%d" % b) for b in range(3)]
        for b in range(3):
            for i in range(blocks):
                cols = slice(b * BANK + i * P, b * BANK + (i + 1) * P)
                nc.tensor.matmul(turned[b][:, i * P : (i + 1) * P], lhsT=base_sb[:, cols], rhs=ident[:],
                                 start=(i == 0), stop=False, is_transpose=True)
        partial = []
        turned_sb = sb.tile([P, 3 * BANK], F32, name="turned_sb", tag="centred")
        for b in range(3):
            for i in range(blocks):
                cols = slice(b * BANK + i * P, b * BANK + (i + 1) * P)
                nc.tensor.matmul(turned[b][:, i * P : (i + 1) * P], lhsT=xs1[:, cols], rhs=ident[:],
                                 start=False, stop=(i == blocks - 1), is_transpose=True)
            nc.scalar.copy(turned_sb[:, b * BANK : (b + 1) * BANK], turned[b][:])
            back = bank((5 + b) % 8, BANK, "back%d" % b)
            for i in range(blocks):
                nc.tensor.transpose(back[:, i * P : (i + 1) * P], turned_sb[:, b * BANK + i * P : b * BANK + (i + 1) * P], ident[:])
            partial.append(back)
        last = row("last")
        nc.gpsimd.tensor_tensor(last[:], xs2[:, 3 * BANK :], base_sb[:, 3 * BANK :], ALU.add)
        partial.append(last)

        results = [sb.tile([P, BANK], F32, name="result%d" % b, tag="centred" if b == 3 else "result%d" % b) for b in range(4)]
        for lo, hi in STORE_CHUNKS:
            b = lo // BANK
            cols = slice(lo - b * BANK, hi - b * BANK)
            nc.vector.tensor_tensor(results[b][:, cols], (xs2 if b < 3 else xs1)[:, lo:hi], partial[b][:, cols], ALU.add)
            nc.sync.dma_start(out=out[:, lo:hi], in_=results[b][:, cols])
